import numpy as np
import ml_dtypes


def mxq(x, axis, fmt="e4m3"):
    dtype, down = {"e4m3": (ml_dtypes.float8_e4m3fn, 7), "e5m2": (ml_dtypes.float8_e5m2, 14)}[fmt]
    v = np.moveaxis(np.asarray(x, np.float32).astype(ml_dtypes.bfloat16).astype(np.float64), axis, -1)
    blocks = v.reshape(v.shape[:-1] + (-1, 32))
    amax = np.abs(blocks).max(-1, keepdims=True)
    byte = np.maximum(np.where(amax > 0, np.frexp(amax)[1] - 1 + 127, 0) - down, 1)
    scale = np.exp2(byte - 127.0)
    codes = (blocks / scale).astype(np.float32).astype(dtype).astype(np.float64)
    return np.moveaxis((codes * scale).reshape(v.shape), -1, axis)


WIDE = False


def mx_kscale(k):
    if not WIDE:
        return np.ones(k)
    levels = np.array([10, -10, 5, -5, 0])
    if k % 512:
        return np.exp2(np.random.permutation(np.resize(levels, k // 32))).repeat(32)
    a = np.empty((k // 512, 16))
    for p in range(k // 512):
        a[p, :8] = np.random.permutation(np.resize(levels, 8))
        for g in range(8):
            far = levels[np.abs(levels - a[p, g]) >= 10]
            a[p, g + 8] = far[np.random.randint(len(far))]
    return np.exp2(a.ravel()).repeat(32)


def f64(x):
    return np.asarray(x).astype(np.float64)


def striped(idx):
    return np.tile(idx.reshape(-1, 16).T, (8, 1)).astype(np.uint16)


def unstriped(offs):
    return offs[:16].T.reshape(-1).astype(np.int64)


def striped8(idx):
    return np.concatenate([x.reshape(-1, 16).T for x in idx]).astype(np.uint16)


def runs(offs, k):
    lists = np.stack([offs[16 * r : 16 * r + 16].T.reshape(-1) for r in range(8)]).astype(np.int64)
    return lists[np.arange(k) % 512 // 64]


def pack_weight(w):
    k, n = w.shape
    w = f64(np.asarray(w, np.float32).astype(ml_dtypes.bfloat16)).reshape(k // 32, 32, n)
    amax = np.abs(w).max(1)
    byte = np.clip(np.where(amax > 0, np.frexp(amax)[1] - 1 + 127 - 7, 1), 1, 254)
    scaled = (w * np.exp2(127.0 - byte)[:, None, :]).reshape(k, n).astype(np.float32)
    words = np.ascontiguousarray(scaled.reshape(k // 512, 128, 4, n).transpose(0, 1, 3, 2)).astype(ml_dtypes.float8_e4m3fn).view(np.uint8)
    return words, np.ascontiguousarray(byte.astype(np.uint8).reshape(k // 512, 16, n))


def unpack_weight(words, scales):
    g, p, n, _ = words.shape
    vals = np.ascontiguousarray(words).view(ml_dtypes.float8_e4m3fn).astype(np.float64) * np.repeat(np.exp2(scales.astype(np.float64) - 127.0), 8, axis=1)[..., None]
    return vals.transpose(0, 1, 3, 2).reshape(g * 512, n)


E2M1 = np.array([0.0, 0.5, 1.0, 1.5, 2.0, 3.0, 4.0, 6.0, -0.0, -0.5, -1.0, -1.5, -2.0, -3.0, -4.0, -6.0])


def pack_fp4(w):
    k, n = w.shape
    w = f64(np.asarray(w, np.float32).astype(ml_dtypes.bfloat16)).reshape(k // 32, 32, n)
    amax = np.abs(w).max(1)
    mant, ex = np.frexp(amax / 6.0)
    byte = np.clip(np.where(amax > 0, np.where(mant > 0.5, ex, ex - 1) + 127, 1), 1, 254)
    scaled = (w * np.exp2(127.0 - byte)[:, None, :]).reshape(k, n).astype(np.float32)
    c = np.ascontiguousarray(scaled.reshape(k // 512, 128, 4, n).transpose(0, 1, 3, 2)).astype(ml_dtypes.float4_e2m1fn).view(np.uint8) & 0xF
    words = (c[..., 0::2] | (c[..., 1::2] << 4)).reshape(k // 512, 128, 2 * n)
    return np.ascontiguousarray(words), np.ascontiguousarray(byte.astype(np.uint8).reshape(k // 512, 16, n))


def unpack_fp4(words, scales):
    g, _, n = scales.shape
    words = np.ascontiguousarray(words).reshape(g, 128, n, 2)
    nib = np.empty((g, 128, n, 4), np.uint8)
    nib[..., 0::2] = words & 0xF
    nib[..., 1::2] = words >> 4
    vals = E2M1[nib] * np.repeat(np.exp2(scales.astype(np.float64) - 127.0), 8, axis=1)[..., None]
    return vals.transpose(0, 1, 3, 2).reshape(g * 512, n)


def planes(y):
    n, m = y.shape
    v = y.astype(np.float32).astype(ml_dtypes.bfloat16).astype(np.float64).reshape(n // 32, 32, m)
    top = np.abs(v).max(1)
    byte = np.clip(np.where(top > 0, np.frexp(top)[1] - 1 + 127 - 7, 1), 1, 254)
    codes = (v * np.exp2(127.0 - byte)[:, None, :]).reshape(n, m).astype(np.float32).astype(ml_dtypes.float8_e4m3fn).view(np.uint8)
    words = codes.reshape(n // 512, 128, 4, m).transpose(0, 1, 3, 2)
    return np.ascontiguousarray(words), np.ascontiguousarray(byte.astype(np.uint8).reshape(n // 512, 16, m))


K, T, S, N, G, H, J = 512, 1024, 512, 512, 2048, 512, 512


def setup_inputs():
    n = np.random.standard_normal
    s = mx_kscale(K)[:, None]
    u = mx_kscale(S)
    packed_xT = pack_weight(n((K, T)) * s)
    packed_dT = pack_weight(n((K, G)) / s)
    packed_w1 = pack_fp4(n((H, N)) / np.sqrt(2 * H) / u[:, None])
    packed_w2 = pack_fp4(n((H, N)) / np.sqrt(2 * H) / u[:, None])
    return {
        "x_words": packed_xT[0],
        "x_scales": packed_xT[1],
        "d_words": packed_dT[0],
        "d_scales": packed_dT[1],
        "tab": n((H, J)).astype(np.float32),
        "gn": (np.random.uniform(0.5, 1.5, (H, 1)) * u[:, None]).astype(np.float32),
        "gm": (np.random.uniform(0.5, 1.5, (H, 1)) * u[:, None]).astype(np.float32),
        "w1_words": packed_w1[0],
        "w1_scales": packed_w1[1],
        "w2_words": packed_w2[0],
        "w2_scales": packed_w2[1],
        "tab2": np.random.uniform(0.4, 1.4, (N, J)).astype(np.float32),
        "offs": striped(np.random.permutation(T)[:S]),
        "k1": striped8(np.random.randint(0, G, (8, H))),
        "two": striped(np.random.permutation(T)[:S]),
        "k2": striped8(np.random.randint(0, G, (8, H))),
        "n1": striped8(np.stack([np.random.permutation(S) for _ in range(8)])),
        "n2": striped8(np.stack([np.random.permutation(S) for _ in range(8)])),
        "n3": striped8(np.random.randint(0, J, (8, S))),
        "n4": striped8(np.random.randint(0, J, (8, S))),
        "n5": striped8(np.stack([np.random.permutation(S) for _ in range(8)])),
        "n6": striped8(np.random.randint(0, J, (8, S))),
        "n7": striped8(np.stack([np.random.permutation(S) for _ in range(8)])),
    }


def reference(x_words, x_scales, d_words, d_scales, tab, gn, gm, w1_words, w1_scales, w2_words, w2_scales, tab2, offs, k1, two, k2, n1, n2, n3, n4, n5, n6, n7):
    d_k1 = unpack_weight(d_words, d_scales)[np.arange(K)[:, None], runs(k1, K)]
    xq = unpack_weight(x_words, x_scales)[:, unstriped(offs)]
    a = 0.0625 * (d_k1.T @ xq)
    st = a + a[np.arange(H)[:, None], runs(n1, H)]
    z = f64(gn) * (st * (np.tanh(st[np.arange(H)[:, None], runs(n2, H)])))
    d_k2 = unpack_weight(d_words, d_scales)[np.arange(K)[:, None], runs(k2, K)]
    x_two = unpack_weight(x_words, x_scales)[:, unstriped(two)]
    b = 0.0625 * (d_k2.T @ x_two)
    z2 = f64(gm) * ((b[np.arange(H)[:, None], runs(n5, H)]) * (f64(tab)[np.arange(H)[:, None], runs(n3, H)]) + f64(tab)[np.arange(H)[:, None], runs(n4, H)])
    h = unpack_fp4(w1_words, w1_scales).T @ mxq(z, 0, "e4m3") + unpack_fp4(w2_words, w2_scales).T @ mxq(z2, 0, "e4m3")
    out_0 = h * (f64(tab2)[np.arange(N)[:, None], runs(n6, N)]) - (0.5 * (h[np.arange(N)[:, None], runs(n7, N)]))
    return (out_0,) + planes(out_0)

@@ -1,0 +1,273 @@
+from contextlib import ExitStack
+
+import concourse.mybir as mybir
+
+F32 = mybir.dt.float32
+BF16 = mybir.dt.bfloat16
+I32 = mybir.dt.int32
+U32 = mybir.dt.uint32
+U16 = mybir.dt.uint16
+U8 = mybir.dt.uint8
+FP8X4 = mybir.dt.float8_e4m3fn_x4
+FP4X4 = mybir.dt.float4_e2m1fn_x4
+ACT = mybir.ActivationFunctionType
+ALU = mybir.AluOpType
+
+P = 128
+PACK = 4
+S = 512
+T = 1024
+G = 2048
+HALF = S // 2
+HCOLS = HALF // 16
+
+FLOPS = 4 * 2 * 512 * 512 * 512
+
+
+def tile_picked_pqjhoppkindakindg_none_po_kernel(
+    tc, x_words, x_scales, d_words, d_scales, tab, gn, gm, w1_words, w1_scales, w2_words, w2_scales, tab2,
+    offs, k1, two, k2, n1, n2, n3, n4, n5, n6, n7, out_0, out_1, out_2,
+):
+    nc = tc.nc
+    with ExitStack() as ctx:
+        keep = ctx.enter_context(tc.tile_pool(name="keep", bufs=1))
+        turns = ctx.enter_context(tc.tile_pool(name="turns", bufs=1))
+        psum = ctx.enter_context(tc.psum_pool(name="psum", bufs=1))
+
+        def sb(name, shape, dtype, tag=None):
+            return keep.tile(shape, dtype, name=name, tag=tag or name, align_bytes=64)
+
+        def load_list(name, src):
+            tile = sb("list_" + name, [P, S // 16], U16)
+            nc.sync.dma_start(tile[:], src)
+            return tile
+
+        def half_of(lst, h):
+            return lst[:, h * HCOLS:(h + 1) * HCOLS]
+
+        def cols(h):
+            return slice(h * HALF, (h + 1) * HALF)
+
+        def zeroed_bytes(name, width, engine, tag=None):
+            tile = sb(name, [P, width], U8, tag=tag)
+            engine.memset(tile[:].bitcast(I32), 0)
+            return tile
+
+        def load_rows(name, src, t, tag=None):
+            tile = sb("%s%d" % (name, t), [P, S], F32, tag=tag)
+            nc.sync.dma_start(tile[:], src.rearrange("(p t) c -> p t c", t=PACK)[:, t, :])
+            return tile
+
+        ds_win = zeroed_bytes("ds_win", G, nc.gpsimd)
+        xs_win = zeroed_bytes("xs_win", T, nc.gpsimd)
+        gm_sb = sb("gm_sb", [P, PACK], F32)
+        nc.gpsimd.dma_start(gm_sb[:], gm.rearrange("(p t) o -> p (t o)", t=PACK))
+        gn_sb = sb("gn_sb", [P, PACK], F32)
+        nc.gpsimd.dma_start(gn_sb[:], gn.rearrange("(p t) o -> p (t o)", t=PACK))
+        placed = zeroed_bytes("placed", 4 * S, nc.vector)
+
+        l_k2 = load_list("k2", k2)
+        nc.sync.dma_start(ds_win[0:P:8, :].bitcast(I32), d_scales[0].bitcast(I32))
+        l_k1 = load_list("k1", k1)
+        nc.sync.dma_start(xs_win[0:P:8, :].bitcast(I32), x_scales[0].bitcast(I32))
+        l_two = load_list("two", two)
+        l_offs = load_list("offs", offs)
+        l_n3 = load_list("n3", n3)
+        tabs = [load_rows("tab", tab, 0)]
+        l_n4 = load_list("n4", n4)
+        xw_win = sb("xw_win", [P, T], I32)
+        nc.sync.dma_start(xw_win[:], x_words[0].rearrange("p c r -> p (c r)").bitcast(I32))
+        tabs.append(load_rows("tab", tab, 1))
+        l_n5 = load_list("n5", n5)
+        l_n1 = load_list("n1", n1)
+        l_n2 = load_list("n2", n2)
+        l_n6 = load_list("n6", n6)
+        dw_win = sb("dw_win", [P, G], I32)
+        nc.sync.dma_start(dw_win[:], d_words[0].rearrange("p c r -> p (c r)").bitcast(I32))
+        tabs.extend([load_rows("tab", tab, t) for t in range(2, PACK)])
+        l_n7 = load_list("n7", n7)
+        gm16 = sb("gm16", [P, PACK], F32)
+        nc.scalar.activation(gm16[:], gm_sb[:], ACT.Copy, scale=0.0625)
+
+        got = turns.tile([P, 4 * S], U8, name="got_bytes", offset=2 * S, align_bytes=64)
+        for i, (win, lst) in enumerate(((ds_win, l_k2), (ds_win, l_k1), (xs_win, l_two), (xs_win, l_offs))):
+            nc.vector.tensor_copy(got[:, i * S:(i + 1) * S], win[:].indirect(lst[:]))
+        for q in range(4):
+            nc.sync.dma_start(placed[32 * q:32 * q + 4, :].bitcast(I32), got[32 * q:32 * q + 32:8, :].bitcast(I32))
+
+        def word_tile(name, i, offset):
+            if i == 0:
+                return sb(name + "0", [P, S], I32)
+            return turns.tile([P, S], I32, name=name + "1", offset=offset, align_bytes=64)
+
+        def coded_product(i, l_d, l_x, tag0):
+            xw = word_tile("xw", i, 0)
+            nc.vector.tensor_copy(xw[:].bitcast(U32), xw_win[:].bitcast(U32).indirect(l_x[:]))
+            dw = word_tile("dw", i, 4 * S)
+            nc.vector.tensor_copy(dw[:].bitcast(U32), dw_win[:].bitcast(U32).indirect(l_d[:]))
+            dw_dealt = sb("dw_dealt%d" % i, [P, S], I32)
+            nc.vector.tensor_copy(
+                dw_dealt[:].bitcast(U32).rearrange("p (t c i) -> p c t i", t=PACK, i=4),
+                dw[:].bitcast(U32).rearrange("p (c i t) -> p c t i", t=PACK, i=4),
+            )
+            ds_dealt = sb("ds_dealt%d" % i, [P, S], U8)
+            nc.vector.tensor_copy(
+                ds_dealt[:].rearrange("p (t m) -> p t m", t=PACK),
+                placed[:, i * S:(i + 1) * S].rearrange("p (m t) -> p t m", t=PACK),
+            )
+            banks = []
+            for t in range(PACK):
+                bank = psum.tile([P, S], F32, name="bank%d_%d" % (i, t), tag="bank%d" % (tag0 + t))
+                nc.tensor.matmul_mx(
+                    out=bank[:],
+                    lhsT=dw_dealt[:, t * P:(t + 1) * P].bitcast(FP8X4),
+                    lhsT_scale=ds_dealt[:, t * P:(t + 1) * P],
+                    rhs=xw[:].bitcast(FP8X4),
+                    rhs_scale=placed[:, (2 + i) * S:(3 + i) * S],
+                    start=True, stop=True,
+                )
+                banks.append(bank)
+            return banks
+
+        def scalar_gather(name, win, lst, tag=None):
+            got = sb(name, [P, S], F32, tag=tag)
+            for h in range(2):
+                nc.scalar.activation(got[:, cols(h)], win[:].indirect(half_of(lst, h)), ACT.Copy)
+            return got
+
+        def round_and_quantize(name, planes, codes, scales, h):
+            woven = sb("%s_woven%d" % (name, h), [P, HALF, PACK], BF16)
+            nc.vector.tensor_copy(
+                woven[:].rearrange("p (c i) t -> p c t i", i=4),
+                planes[:].rearrange("p t (c i) -> p c t i", i=4),
+            )
+            nc.vector.quantize_mx(
+                out=codes[:, cols(h)].bitcast(FP8X4), scales=scales[:, cols(h)],
+                in_=woven[:].rearrange("p c t -> p (c t)"),
+            )
+
+        t3 = []
+        t4 = []
+        for t in range(PACK):
+            t3.append(scalar_gather("t3_%d" % t, tabs[t], l_n3, tag="t3t6_%d" % t))
+            if t < 2:
+                t4.append(scalar_gather("t4_%d" % t, tabs[t], l_n4))
+        b_banks = coded_product(0, l_k2, l_two, PACK)
+
+        gn16 = sb("gn16", [P, PACK], F32)
+        nc.vector.tensor_scalar(gn16[:], gn_sb[:], 0.0625, None, ALU.mult)
+        gn_safe = sb("gn_safe", [P, PACK], F32)
+        nc.vector.scalar_tensor_tensor(gn_safe[:], gn_sb[:], 0.0, gn_sb[:], ALU.is_equal, ALU.add)
+        gn_inv = sb("gn_inv", [P, PACK], F32)
+        nc.vector.reciprocal(gn_inv[:], gn_safe[:])
+
+        a_banks = coded_product(1, l_k1, l_offs, 0)
+
+        def scaled_rows(name, bank, gain):
+            rows = sb(name, [P, S], F32)
+            nc.scalar.activation(rows[:], bank[:], ACT.Copy, scale=gain)
+            return rows
+
+        gb = [scaled_rows("gb%d" % t, b_banks[t], gm16[:, t:t + 1]) for t in range(PACK)]
+        bt = []
+        for t in range(PACK):
+            bt_t = sb("bt%d" % t, [P, S], F32)
+            for h in range(2):
+                nc.vector.tensor_tensor(bt_t[:, cols(h)], gb[t][:].indirect(half_of(l_n5, h)), t3[t][:, cols(h)], ALU.mult)
+            bt.append(bt_t)
+        ww_raw = sb("ww_raw", [P, 2, 2 * S], U8, tag="dw_win")
+        for i, words in enumerate((w1_words, w2_words)):
+            nc.sync.dma_start(ww_raw[:, i, :].bitcast(I32), words[0].bitcast(I32))
+        ws_raw = zeroed_bytes("ws_raw", 2 * S, nc.gpsimd, tag="gb3")
+        for i, scales in enumerate((w1_scales, w2_scales)):
+            for q in range(4):
+                nc.sync.dma_start(
+                    ws_raw[32 * q:32 * q + 4, i * S:(i + 1) * S].bitcast(I32), scales[0, 4 * q:4 * q + 4, :].bitcast(I32))
+
+        z2_codes = sb("z2_codes", [P, S], I32)
+        z2_scales = sb("z2_scales", [P, S], U8)
+        z2 = [sb("z2_%d" % h, [P, PACK, HALF], F32) for h in range(2)]
+        st = []
+        th = []
+        tab2s = []
+        for t in range(PACK):
+            ga = scaled_rows("ga%d" % t, a_banks[t], gn16[:, t:t + 1])
+            ga1 = scalar_gather("ga1_%d" % t, ga, l_n1)
+            if t < 2:
+                t4.append(scalar_gather("t4_%d" % (t + 2), tabs[t + 2], l_n4, tag=("dw_dealt1", "placed")[t]))
+            for h in range(2):
+                nc.vector.scalar_tensor_tensor(
+                    z2[h][:, t, :], t4[t][:, cols(h)], gm_sb[:, t:t + 1], bt[t][:, cols(h)], ALU.mult, ALU.add)
+            gst = sb("gst%d" % t, [P, S], F32)
+            nc.vector.tensor_tensor(gst[:], ga[:], ga1[:], ALU.add)
+            st.append(gst)
+            tab2s.append(load_rows("tab2_", tab2, t, tag="ga1_%d" % t))
+            tanh_t = sb("th%d" % t, [P, S], F32)
+            nc.scalar.activation(tanh_t[:], gst[:], ACT.Tanh, scale=gn_inv[:, t:t + 1])
+            th.append(tanh_t)
+        for h in range(2):
+            round_and_quantize("z2", z2[h], z2_codes, z2_scales, h)
+
+        ww = sb("ww", [P, 2, 2 * S], U8)
+        for i in range(2):
+            nc.scalar.copy(
+                ww[:, i, :].bitcast(U16).rearrange("p (t m) -> p t m", t=PACK),
+                ww_raw[:, i, :].bitcast(U16).rearrange("p (m t) -> p t m", t=PACK),
+            )
+        ws = sb("ws", [P, 2 * S], U8)
+        nc.vector.tensor_copy(
+            ws[:].rearrange("p (w t m) -> p w t m", w=2, t=PACK),
+            ws_raw[:].rearrange("p (w m t) -> p w t m", w=2, t=PACK),
+        )
+
+        h_banks = [psum.tile([P, S], F32, name="hbank%d" % t, tag="bank%d" % t) for t in range(PACK)]
+
+        def weight_pass(t, i, codes, scales, span, start, stop):
+            nc.tensor.matmul_mx(
+                out=h_banks[t][:, span],
+                lhsT=ww[:, i, 2 * P * t:2 * P * (t + 1)].bitcast(FP4X4),
+                lhsT_scale=ws[:, i * S + P * t:i * S + P * (t + 1)],
+                rhs=codes[:, span].bitcast(FP8X4),
+                rhs_scale=scales[:, span],
+                start=start, stop=stop,
+            )
+
+        for t in range(PACK):
+            weight_pass(t, 1, z2_codes, z2_scales, slice(0, S), True, False)
+
+        t6 = [scalar_gather("t6_%d" % t, tab2s[t], l_n6, tag="t3t6_%d" % t) for t in range(PACK)]
+
+        z_codes = sb("z_codes", [P, S], I32)
+        z_scales = sb("z_scales", [P, S], U8)
+        for h in range(2):
+            z = sb("z_%d" % h, [P, PACK, HALF], F32)
+            for t in range(PACK):
+                nc.vector.tensor_tensor(z[:, t, :], th[t][:].indirect(half_of(l_n2, h)), st[t][:, cols(h)], ALU.mult)
+            round_and_quantize("z", z, z_codes, z_scales, h)
+            for t in range(PACK):
+                weight_pass(t, 0, z_codes, z_scales, cols(h), False, h == 1)
+
+        hm = []
+        ht = []
+        for t in range(PACK):
+            hm_t = sb("hm%d" % t, [P, S], F32)
+            nc.scalar.activation(hm_t[:], h_banks[t][:], ACT.Copy, scale=-0.5)
+            hm.append(hm_t)
+            ht_t = sb("ht%d" % t, [P, S], F32)
+            nc.vector.scalar_tensor_tensor(ht_t[:], t6[t][:], -2.0, hm_t[:], ALU.mult, ALU.mult)
+            ht.append(ht_t)
+        o_codes = sb("o_codes", [P, S], I32)
+        o_scales = sb("o_scales", [P, S], U8)
+        out_rows = out_0.rearrange("(p t) c -> p t c", t=PACK)
+        words_out = out_1[0].rearrange("p c r -> p (c r)").bitcast(I32)
+        for h in range(2):
+            o = sb("o_%d" % h, [P, PACK, HALF], F32)
+            for t in range(PACK):
+                h7 = sb("h7_%d_%d" % (h, t), [P, HALF], F32)
+                nc.scalar.activation(h7[:], hm[t][:].indirect(half_of(l_n7, h)), ACT.Copy)
+                nc.vector.tensor_tensor(o[:, t, :], h7[:], ht[t][:, cols(h)], ALU.add)
+            nc.sync.dma_start(out_rows[:, :, cols(h)], o[:])
+            round_and_quantize("o", o, o_codes, o_scales, h)
+            nc.sync.dma_start(words_out[:, cols(h)], o_codes[:, cols(h)])
+        for q in range(4):
+            nc.sync.dma_start(out_2[0, 4 * q:4 * q + 4, :].bitcast(I32), o_scales[32 * q:32 * q + 4, :].bitcast(I32))

@@ -31,7 +31,6 @@ def tile_picked_pqjhoppkindakindg_none_po_kernel(
     nc = tc.nc
     with ExitStack() as ctx:
         keep = ctx.enter_context(tc.tile_pool(name="keep", bufs=1))
-        turns = ctx.enter_context(tc.tile_pool(name="turns", bufs=1))
         psum = ctx.enter_context(tc.psum_pool(name="psum", bufs=1))
 
         def sb(name, shape, dtype, tag=None):
@@ -54,8 +53,8 @@ def tile_picked_pqjhoppkindakindg_none_po_kernel(
             return tile
 
         def load_rows(name, src, t, tag=None):
-            tile = sb("%s%d" % (name, t), [P, S], F32, tag=tag)
-            nc.sync.dma_start(tile[:], src.rearrange("(p t) c -> p t c", t=PACK)[:, t, :])
+            tile = sb("%s%d" % (name, t), [P, 2 * S], F32, tag=tag)
+            nc.sync.dma_start(tile[:, 0:S], src.rearrange("(p t) c -> p t c", t=PACK)[:, t, :])
             return tile
 
         ds_win = zeroed_bytes("ds_win", G, nc.gpsimd)
@@ -64,48 +63,45 @@ def tile_picked_pqjhoppkindakindg_none_po_kernel(
         nc.gpsimd.dma_start(gm_sb[:], gm.rearrange("(p t) o -> p (t o)", t=PACK))
         gn_sb = sb("gn_sb", [P, PACK], F32)
         nc.gpsimd.dma_start(gn_sb[:], gn.rearrange("(p t) o -> p (t o)", t=PACK))
-        placed = zeroed_bytes("placed", 4 * S, nc.vector)
 
         l_k2 = load_list("k2", k2)
         nc.sync.dma_start(ds_win[0:P:8, :].bitcast(I32), d_scales[0].bitcast(I32))
-        l_k1 = load_list("k1", k1)
         nc.sync.dma_start(xs_win[0:P:8, :].bitcast(I32), x_scales[0].bitcast(I32))
-        l_two = load_list("two", two)
-        l_offs = load_list("offs", offs)
+        l_k1 = load_list("k1", k1)
         l_n3 = load_list("n3", n3)
-        tabs = [load_rows("tab", tab, 0)]
         l_n4 = load_list("n4", n4)
+        l_two = load_list("two", two)
+        tabs = [load_rows("tab", tab, t) for t in range(2)]
+        l_offs = load_list("offs", offs)
         xw_win = sb("xw_win", [P, T], I32)
         nc.sync.dma_start(xw_win[:], x_words[0].rearrange("p c r -> p (c r)").bitcast(I32))
-        tabs.append(load_rows("tab", tab, 1))
+        tabs.extend([load_rows("tab", tab, t) for t in range(2, PACK)])
         l_n5 = load_list("n5", n5)
         l_n1 = load_list("n1", n1)
-        l_n2 = load_list("n2", n2)
-        l_n6 = load_list("n6", n6)
         dw_win = sb("dw_win", [P, G], I32)
         nc.sync.dma_start(dw_win[:], d_words[0].rearrange("p c r -> p (c r)").bitcast(I32))
-        tabs.extend([load_rows("tab", tab, t) for t in range(2, PACK)])
+        l_n2 = load_list("n2", n2)
+        l_n6 = load_list("n6", n6)
         l_n7 = load_list("n7", n7)
+        for t in (0, 2, 3):
+            nc.vector.memset(tabs[t][:, S:2 * S], 0.0)
+        nc.scalar.activation(tabs[1][:, S:2 * S], tabs[0][:, S:2 * S], ACT.Copy)
+        placed = zeroed_bytes("placed", 4 * S, nc.vector)
         gm16 = sb("gm16", [P, PACK], F32)
-        nc.scalar.activation(gm16[:], gm_sb[:], ACT.Copy, scale=0.0625)
+        nc.gpsimd.tensor_scalar(gm16[:], gm_sb[:], 0.0625, 0.0, ALU.mult, ALU.add)
 
-        got = turns.tile([P, 4 * S], U8, name="got_bytes", offset=2 * S, align_bytes=64)
+        got = sb("got_bytes", [P, 4 * S], U8)
         for i, (win, lst) in enumerate(((ds_win, l_k2), (ds_win, l_k1), (xs_win, l_two), (xs_win, l_offs))):
             nc.vector.tensor_copy(got[:, i * S:(i + 1) * S], win[:].indirect(lst[:]))
         for q in range(4):
             nc.sync.dma_start(placed[32 * q:32 * q + 4, :].bitcast(I32), got[32 * q:32 * q + 32:8, :].bitcast(I32))
 
-        def word_tile(name, i, offset):
-            if i == 0:
-                return sb(name + "0", [P, S], I32)
-            return turns.tile([P, S], I32, name=name + "1", offset=offset, align_bytes=64)
-
         def coded_product(i, l_d, l_x, tag0):
-            xw = word_tile("xw", i, 0)
+            xw = sb("xw%d" % i, [P, S], I32)
             nc.vector.tensor_copy(xw[:].bitcast(U32), xw_win[:].bitcast(U32).indirect(l_x[:]))
-            dw = word_tile("dw", i, 4 * S)
+            dw = sb("dw%d" % i, [P, S], I32, tag="dw")
             nc.vector.tensor_copy(dw[:].bitcast(U32), dw_win[:].bitcast(U32).indirect(l_d[:]))
-            dw_dealt = sb("dw_dealt%d" % i, [P, S], I32)
+            dw_dealt = sb("dw_dealt%d" % i, [P, S], I32, tag=("got_bytes", "dw_dealt1")[i])
             nc.vector.tensor_copy(
                 dw_dealt[:].bitcast(U32).rearrange("p (t c i) -> p c t i", t=PACK, i=4),
                 dw[:].bitcast(U32).rearrange("p (c i t) -> p c t i", t=PACK, i=4),
@@ -129,84 +125,73 @@ def tile_picked_pqjhoppkindakindg_none_po_kernel(
                 banks.append(bank)
             return banks
 
-        def scalar_gather(name, win, lst, tag=None):
-            got = sb(name, [P, S], F32, tag=tag)
-            for h in range(2):
-                nc.scalar.activation(got[:, cols(h)], win[:].indirect(half_of(lst, h)), ACT.Copy)
-            return got
+        def scalar_gather(out, win, lst):
+            nc.scalar.activation(out, win[:].indirect(lst), ACT.Copy)
 
-        def round_and_quantize(name, planes, codes, scales, h):
-            woven = sb("%s_woven%d" % (name, h), [P, HALF, PACK], BF16)
-            nc.vector.tensor_copy(
+        def round_and_quantize(name, planes, codes, scales, span, copy):
+            woven = sb(name + "_woven", [P, HALF, PACK], BF16)
+            copy(
                 woven[:].rearrange("p (c i) t -> p c t i", i=4),
-                planes[:].rearrange("p t (c i) -> p c t i", i=4),
+                planes.rearrange("p t (c i) -> p c t i", i=4),
             )
             nc.vector.quantize_mx(
-                out=codes[:, cols(h)].bitcast(FP8X4), scales=scales[:, cols(h)],
+                out=codes[:, span].bitcast(FP8X4), scales=scales[:, span],
                 in_=woven[:].rearrange("p c t -> p (c t)"),
             )
 
-        t3 = []
-        t4 = []
+        rest = slice(S, 2 * S)
+        gb = [sb("gb%d" % t, [P, 2 * S], F32) for t in range(PACK)]
+        t3 = [gb[(t - 1) % PACK][:, rest] for t in range(PACK)]
+        ga = [sb("ga%d" % t, [P, 2 * S], F32) for t in range(PACK)]
         for t in range(PACK):
-            t3.append(scalar_gather("t3_%d" % t, tabs[t], l_n3, tag="t3t6_%d" % t))
-            if t < 2:
-                t4.append(scalar_gather("t4_%d" % t, tabs[t], l_n4))
+            scalar_gather(t3[t], tabs[t], l_n3[:])
+            scalar_gather(ga[t][:, rest], tabs[t], l_n4[:])
         b_banks = coded_product(0, l_k2, l_two, PACK)
 
         gn16 = sb("gn16", [P, PACK], F32)
-        nc.vector.tensor_scalar(gn16[:], gn_sb[:], 0.0625, None, ALU.mult)
-        gn_safe = sb("gn_safe", [P, PACK], F32)
-        nc.vector.scalar_tensor_tensor(gn_safe[:], gn_sb[:], 0.0, gn_sb[:], ALU.is_equal, ALU.add)
-        gn_inv = sb("gn_inv", [P, PACK], F32)
-        nc.vector.reciprocal(gn_inv[:], gn_safe[:])
+        nc.gpsimd.tensor_scalar(gn16[:], gn_sb[:], 0.0625, 0.0, ALU.mult, ALU.add)
 
         a_banks = coded_product(1, l_k1, l_offs, 0)
 
-        def scaled_rows(name, bank, gain):
-            rows = sb(name, [P, S], F32)
-            nc.scalar.activation(rows[:], bank[:], ACT.Copy, scale=gain)
-            return rows
-
-        gb = [scaled_rows("gb%d" % t, b_banks[t], gm16[:, t:t + 1]) for t in range(PACK)]
+        for t in range(PACK):
+            nc.scalar.activation(gb[t][:, 0:S], b_banks[t][:], ACT.Copy, scale=gm16[:, t:t + 1])
         bt = []
         for t in range(PACK):
             bt_t = sb("bt%d" % t, [P, S], F32)
-            for h in range(2):
-                nc.vector.tensor_tensor(bt_t[:, cols(h)], gb[t][:].indirect(half_of(l_n5, h)), t3[t][:, cols(h)], ALU.mult)
+            nc.vector.tensor_tensor(bt_t[:], gb[t][:].indirect(l_n5[:]), t3[t], ALU.mult)
             bt.append(bt_t)
         ww_raw = sb("ww_raw", [P, 2, 2 * S], U8, tag="dw_win")
         for i, words in enumerate((w1_words, w2_words)):
             nc.sync.dma_start(ww_raw[:, i, :].bitcast(I32), words[0].bitcast(I32))
-        ws_raw = zeroed_bytes("ws_raw", 2 * S, nc.gpsimd, tag="gb3")
+        ws_raw = zeroed_bytes("ws_raw", 2 * S, nc.gpsimd, tag="dw")
         for i, scales in enumerate((w1_scales, w2_scales)):
             for q in range(4):
                 nc.sync.dma_start(
                     ws_raw[32 * q:32 * q + 4, i * S:(i + 1) * S].bitcast(I32), scales[0, 4 * q:4 * q + 4, :].bitcast(I32))
 
+        gn_safe = sb("gn_safe", [P, PACK], F32, tag="ds_dealt1")
+        nc.vector.scalar_tensor_tensor(gn_safe[:], gn_sb[:], 0.0, gn_sb[:], ALU.is_equal, ALU.add)
+        gn_inv = sb("gn_inv", [P, PACK], F32)
+        nc.vector.reciprocal(gn_inv[:], gn_safe[:])
+
         z2_codes = sb("z2_codes", [P, S], I32)
         z2_scales = sb("z2_scales", [P, S], U8)
-        z2 = [sb("z2_%d" % h, [P, PACK, HALF], F32) for h in range(2)]
-        st = []
+        z2 = sb("z2", [P, PACK, S], F32)
         th = []
         tab2s = []
         for t in range(PACK):
-            ga = scaled_rows("ga%d" % t, a_banks[t], gn16[:, t:t + 1])
-            ga1 = scalar_gather("ga1_%d" % t, ga, l_n1)
-            if t < 2:
-                t4.append(scalar_gather("t4_%d" % (t + 2), tabs[t + 2], l_n4, tag=("dw_dealt1", "placed")[t]))
-            for h in range(2):
-                nc.vector.scalar_tensor_tensor(
-                    z2[h][:, t, :], t4[t][:, cols(h)], gm_sb[:, t:t + 1], bt[t][:, cols(h)], ALU.mult, ALU.add)
-            gst = sb("gst%d" % t, [P, S], F32)
-            nc.vector.tensor_tensor(gst[:], ga[:], ga1[:], ALU.add)
-            st.append(gst)
-            tab2s.append(load_rows("tab2_", tab2, t, tag="ga1_%d" % t))
+            nc.scalar.activation(ga[t][:, 0:S], a_banks[t][:], ACT.Copy, scale=gn16[:, t:t + 1])
+            ga1 = sb("ga1_%d" % t, [P, S], F32)
+            scalar_gather(ga1[:], ga[t], l_n1[:])
+            nc.vector.scalar_tensor_tensor(z2[:, t, :], ga[t][:, rest], gm_sb[:, t:t + 1], bt[t][:], ALU.mult, ALU.add)
+            tab2s.append(load_rows("tab2_", tab2, t, tag=("xw0", "ds_dealt0", "got_bytes", "xw1")[t]))
+            gst = tab2s[t][:, rest]
+            nc.vector.tensor_tensor(gst, ga[t][:, 0:S], ga1[:], ALU.add)
             tanh_t = sb("th%d" % t, [P, S], F32)
-            nc.scalar.activation(tanh_t[:], gst[:], ACT.Tanh, scale=gn_inv[:, t:t + 1])
+            nc.scalar.activation(tanh_t[:], gst, ACT.Tanh, scale=gn_inv[:, t:t + 1])
             th.append(tanh_t)
-        for h in range(2):
-            round_and_quantize("z2", z2[h], z2_codes, z2_scales, h)
+        for h, copy in enumerate((nc.vector.tensor_copy, nc.scalar.copy)):
+            round_and_quantize("z2_%d" % h, z2[:, :, cols(h)], z2_codes, z2_scales, cols(h), copy)
 
         ww = sb("ww", [P, 2, 2 * S], U8)
         for i in range(2):
@@ -220,54 +205,64 @@ def tile_picked_pqjhoppkindakindg_none_po_kernel(
             ws_raw[:].rearrange("p (w m t) -> p w t m", w=2, t=PACK),
         )
 
-        h_banks = [psum.tile([P, S], F32, name="hbank%d" % t, tag="bank%d" % t) for t in range(PACK)]
+        h_banks = [
+            [psum.tile([P, HALF], F32, name="hbank%d_%d" % (h, t), tag="bank%d" % (PACK * (1 - h) + t)) for t in range(PACK)]
+            for h in range(2)
+        ]
 
-        def weight_pass(t, i, codes, scales, span, start, stop):
+        def weight_pass(t, h, i, codes, scales, first):
             nc.tensor.matmul_mx(
-                out=h_banks[t][:, span],
+                out=h_banks[h][t][:],
                 lhsT=ww[:, i, 2 * P * t:2 * P * (t + 1)].bitcast(FP4X4),
                 lhsT_scale=ws[:, i * S + P * t:i * S + P * (t + 1)],
-                rhs=codes[:, span].bitcast(FP8X4),
-                rhs_scale=scales[:, span],
-                start=start, stop=stop,
+                rhs=codes[:, cols(h)].bitcast(FP8X4),
+                rhs_scale=scales[:, cols(h)],
+                start=first, stop=not first,
             )
 
-        for t in range(PACK):
-            weight_pass(t, 1, z2_codes, z2_scales, slice(0, S), True, False)
+        for h in range(2):
+            for t in range(PACK):
+                weight_pass(t, h, 1, z2_codes, z2_scales, True)
 
-        t6 = [scalar_gather("t6_%d" % t, tab2s[t], l_n6, tag="t3t6_%d" % t) for t in range(PACK)]
+        t6 = []
+        for t in range(PACK):
+            t6_t = sb("t6_%d" % t, [P, S], F32)
+            scalar_gather(t6_t[:], tab2s[t], l_n6[:])
+            t6.append(t6_t)
 
         z_codes = sb("z_codes", [P, S], I32)
         z_scales = sb("z_scales", [P, S], U8)
+        hm = [sb("hm%d" % t, [P, S], F32) for t in range(PACK)]
+        ht = [sb("ht%d" % h, [P, PACK, HALF], F32) for h in range(2)]
         for h in range(2):
             z = sb("z_%d" % h, [P, PACK, HALF], F32)
             for t in range(PACK):
-                nc.vector.tensor_tensor(z[:, t, :], th[t][:].indirect(half_of(l_n2, h)), st[t][:, cols(h)], ALU.mult)
-            round_and_quantize("z", z, z_codes, z_scales, h)
+                nc.vector.tensor_tensor(
+                    z[:, t, :], th[t][:].indirect(half_of(l_n2, h)), tab2s[t][:, S + h * HALF:S + (h + 1) * HALF], ALU.mult)
+            round_and_quantize("z%d" % h, z[:], z_codes, z_scales, cols(h), nc.vector.tensor_copy)
             for t in range(PACK):
-                weight_pass(t, 0, z_codes, z_scales, cols(h), False, h == 1)
+                weight_pass(t, h, 0, z_codes, z_scales, False)
+                nc.scalar.activation(hm[t][:, cols(h)], h_banks[h][t][:], ACT.Copy, scale=-0.5)
+        for h in range(2):
+            for t in range(PACK):
+                nc.vector.scalar_tensor_tensor(
+                    ht[h][:, t, :], t6[t][:, cols(h)], -2.0, hm[t][:, cols(h)], ALU.mult, ALU.mult)
 
-        hm = []
-        ht = []
-        for t in range(PACK):
-            hm_t = sb("hm%d" % t, [P, S], F32)
-            nc.scalar.activation(hm_t[:], h_banks[t][:], ACT.Copy, scale=-0.5)
-            hm.append(hm_t)
-            ht_t = sb("ht%d" % t, [P, S], F32)
-            nc.vector.scalar_tensor_tensor(ht_t[:], t6[t][:], -2.0, hm_t[:], ALU.mult, ALU.mult)
-            ht.append(ht_t)
         o_codes = sb("o_codes", [P, S], I32)
         o_scales = sb("o_scales", [P, S], U8)
         out_rows = out_0.rearrange("(p t) c -> p t c", t=PACK)
         words_out = out_1[0].rearrange("p c r -> p (c r)").bitcast(I32)
         for h in range(2):
             o = sb("o_%d" % h, [P, PACK, HALF], F32)
-            for t in range(PACK):
-                h7 = sb("h7_%d_%d" % (h, t), [P, HALF], F32)
-                nc.scalar.activation(h7[:], hm[t][:].indirect(half_of(l_n7, h)), ACT.Copy)
-                nc.vector.tensor_tensor(o[:, t, :], h7[:], ht[t][:, cols(h)], ALU.add)
+            by_scalar = (PACK, 3)[h]
+            h7 = sb("h7_%d" % h, [P, by_scalar, HALF], F32)
+            for t in range(by_scalar):
+                scalar_gather(h7[:, t, :], hm[t], half_of(l_n7, h))
+            for t in range(by_scalar, PACK):
+                nc.vector.tensor_tensor(o[:, t, :], hm[t][:].indirect(half_of(l_n7, h)), ht[h][:, t, :], ALU.add)
+            nc.vector.tensor_tensor(o[:, 0:by_scalar, :], h7[:], ht[h][:, 0:by_scalar, :], ALU.add)
             nc.sync.dma_start(out_rows[:, :, cols(h)], o[:])
-            round_and_quantize("o", o, o_codes, o_scales, h)
+            round_and_quantize("o%d" % h, o[:], o_codes, o_scales, cols(h), (nc.scalar.copy, nc.vector.tensor_copy)[h])
             nc.sync.dma_start(words_out[:, cols(h)], o_codes[:, cols(h)])
         for q in range(4):
             nc.sync.dma_start(out_2[0, 4 * q:4 * q + 4, :].bitcast(I32), o_scales[32 * q:32 * q + 4, :].bitcast(I32))

@@ -254,7 +254,7 @@ def tile_picked_pqjhoppkindakindg_none_po_kernel(
         words_out = out_1[0].rearrange("p c r -> p (c r)").bitcast(I32)
         for h in range(2):
             o = sb("o_%d" % h, [P, PACK, HALF], F32)
-            by_scalar = (PACK, 3)[h]
+            by_scalar = (3, 2)[h]
             h7 = sb("h7_%d" % h, [P, by_scalar, HALF], F32)
             for t in range(by_scalar):
                 scalar_gather(h7[:, t, :], hm[t], half_of(l_n7, h))

from contextlib import ExitStack

import concourse.mybir as mybir

F32 = mybir.dt.float32
BF16 = mybir.dt.bfloat16
I32 = mybir.dt.int32
U32 = mybir.dt.uint32
U16 = mybir.dt.uint16
U8 = mybir.dt.uint8
FP8X4 = mybir.dt.float8_e4m3fn_x4
FP4X4 = mybir.dt.float4_e2m1fn_x4
ACT = mybir.ActivationFunctionType
ALU = mybir.AluOpType

P = 128
PACK = 4
S = 512
T = 1024
G = 2048
HALF = S // 2
HCOLS = HALF // 16

FLOPS = 4 * 2 * 512 * 512 * 512


def tile_picked_pqjhoppkindakindg_none_po_kernel(
    tc, x_words, x_scales, d_words, d_scales, tab, gn, gm, w1_words, w1_scales, w2_words, w2_scales, tab2,
    offs, k1, two, k2, n1, n2, n3, n4, n5, n6, n7, out_0, out_1, out_2,
):
    nc = tc.nc
    with ExitStack() as ctx:
        keep = ctx.enter_context(tc.tile_pool(name="keep", bufs=1))
        psum = ctx.enter_context(tc.psum_pool(name="psum", bufs=1))

        def sb(name, shape, dtype, tag=None):
            return keep.tile(shape, dtype, name=name, tag=tag or name, align_bytes=64)

        def load_list(name, src):
            tile = sb("list_" + name, [P, S // 16], U16)
            nc.sync.dma_start(tile[:], src)
            return tile

        def half_of(lst, h):
            return lst[:, h * HCOLS:(h + 1) * HCOLS]

        def cols(h):
            return slice(h * HALF, (h + 1) * HALF)

        def zeroed_bytes(name, width, engine, tag=None):
            tile = sb(name, [P, width], U8, tag=tag)
            engine.memset(tile[:].bitcast(I32), 0)
            return tile

        def load_rows(name, src, t, tag=None):
            tile = sb("%s%d" % (name, t), [P, 2 * S], F32, tag=tag)
            nc.sync.dma_start(tile[:, 0:S], src.rearrange("(p t) c -> p t c", t=PACK)[:, t, :])
            return tile

        ds_win = zeroed_bytes("ds_win", G, nc.gpsimd)
        xs_win = zeroed_bytes("xs_win", T, nc.gpsimd)
        gm_sb = sb("gm_sb", [P, PACK], F32)
        nc.gpsimd.dma_start(gm_sb[:], gm.rearrange("(p t) o -> p (t o)", t=PACK))
        gn_sb = sb("gn_sb", [P, PACK], F32)
        nc.gpsimd.dma_start(gn_sb[:], gn.rearrange("(p t) o -> p (t o)", t=PACK))

        l_k2 = load_list("k2", k2)
        nc.sync.dma_start(ds_win[0:P:8, :].bitcast(I32), d_scales[0].bitcast(I32))
        nc.sync.dma_start(xs_win[0:P:8, :].bitcast(I32), x_scales[0].bitcast(I32))
        l_k1 = load_list("k1", k1)
        l_n3 = load_list("n3", n3)
        l_n4 = load_list("n4", n4)
        l_two = load_list("two", two)
        tabs = [load_rows("tab", tab, t) for t in range(2)]
        l_offs = load_list("offs", offs)
        xw_win = sb("xw_win", [P, T], I32)
        nc.sync.dma_start(xw_win[:], x_words[0].rearrange("p c r -> p (c r)").bitcast(I32))
        tabs.extend([load_rows("tab", tab, t) for t in range(2, PACK)])
        l_n5 = load_list("n5", n5)
        l_n1 = load_list("n1", n1)
        dw_win = sb("dw_win", [P, G], I32)
        nc.sync.dma_start(dw_win[:], d_words[0].rearrange("p c r -> p (c r)").bitcast(I32))
        l_n2 = load_list("n2", n2)
        l_n6 = load_list("n6", n6)
        l_n7 = load_list("n7", n7)
        for t in (0, 2, 3):
            nc.vector.memset(tabs[t][:, S:2 * S], 0.0)
        nc.scalar.activation(tabs[1][:, S:2 * S], tabs[0][:, S:2 * S], ACT.Copy)
        placed = zeroed_bytes("placed", 4 * S, nc.vector)
        gm16 = sb("gm16", [P, PACK], F32)
        nc.gpsimd.tensor_scalar(gm16[:], gm_sb[:], 0.0625, 0.0, ALU.mult, ALU.add)

        got = sb("got_bytes", [P, 4 * S], U8)
        for i, (win, lst) in enumerate(((ds_win, l_k2), (ds_win, l_k1), (xs_win, l_two), (xs_win, l_offs))):
            nc.vector.tensor_copy(got[:, i * S:(i + 1) * S], win[:].indirect(lst[:]))
        for q in range(4):
            nc.sync.dma_start(placed[32 * q:32 * q + 4, :].bitcast(I32), got[32 * q:32 * q + 32:8, :].bitcast(I32))

        def coded_product(i, l_d, l_x, tag0):
            xw = sb("xw%d" % i, [P, S], I32)
            nc.vector.tensor_copy(xw[:].bitcast(U32), xw_win[:].bitcast(U32).indirect(l_x[:]))
            dw = sb("dw%d" % i, [P, S], I32, tag="dw")
            nc.vector.tensor_copy(dw[:].bitcast(U32), dw_win[:].bitcast(U32).indirect(l_d[:]))
            dw_dealt = sb("dw_dealt%d" % i, [P, S], I32, tag=("got_bytes", "dw_dealt1")[i])
            nc.vector.tensor_copy(
                dw_dealt[:].bitcast(U32).rearrange("p (t c i) -> p c t i", t=PACK, i=4),
                dw[:].bitcast(U32).rearrange("p (c i t) -> p c t i", t=PACK, i=4),
            )
            ds_dealt = sb("ds_dealt%d" % i, [P, S], U8)
            nc.vector.tensor_copy(
                ds_dealt[:].rearrange("p (t m) -> p t m", t=PACK),
                placed[:, i * S:(i + 1) * S].rearrange("p (m t) -> p t m", t=PACK),
            )
            banks = []
            for t in range(PACK):
                bank = psum.tile([P, S], F32, name="bank%d_%d" % (i, t), tag="bank%d" % (tag0 + t))
                nc.tensor.matmul_mx(
                    out=bank[:],
                    lhsT=dw_dealt[:, t * P:(t + 1) * P].bitcast(FP8X4),
                    lhsT_scale=ds_dealt[:, t * P:(t + 1) * P],
                    rhs=xw[:].bitcast(FP8X4),
                    rhs_scale=placed[:, (2 + i) * S:(3 + i) * S],
                    start=True, stop=True,
                )
                banks.append(bank)
            return banks

        def scalar_gather(out, win, lst):
            nc.scalar.activation(out, win[:].indirect(lst), ACT.Copy)

        def round_and_quantize(name, planes, codes, scales, span, copy):
            woven = sb(name + "_woven", [P, HALF, PACK], BF16)
            copy(
                woven[:].rearrange("p (c i) t -> p c t i", i=4),
                planes.rearrange("p t (c i) -> p c t i", i=4),
            )
            nc.vector.quantize_mx(
                out=codes[:, span].bitcast(FP8X4), scales=scales[:, span],
                in_=woven[:].rearrange("p c t -> p (c t)"),
            )

        rest = slice(S, 2 * S)
        gb = [sb("gb%d" % t, [P, 2 * S], F32) for t in range(PACK)]
        t3 = [gb[(t - 1) % PACK][:, rest] for t in range(PACK)]
        ga = [sb("ga%d" % t, [P, 2 * S], F32) for t in range(PACK)]
        for t in range(PACK):
            scalar_gather(t3[t], tabs[t], l_n3[:])
            scalar_gather(ga[t][:, rest], tabs[t], l_n4[:])
        b_banks = coded_product(0, l_k2, l_two, PACK)

        gn16 = sb("gn16", [P, PACK], F32)
        nc.gpsimd.tensor_scalar(gn16[:], gn_sb[:], 0.0625, 0.0, ALU.mult, ALU.add)

        a_banks = coded_product(1, l_k1, l_offs, 0)

        for t in range(PACK):
            nc.scalar.activation(gb[t][:, 0:S], b_banks[t][:], ACT.Copy, scale=gm16[:, t:t + 1])
        bt = []
        for t in range(PACK):
            bt_t = sb("bt%d" % t, [P, S], F32)
            nc.vector.tensor_tensor(bt_t[:], gb[t][:].indirect(l_n5[:]), t3[t], ALU.mult)
            bt.append(bt_t)
        ww_raw = sb("ww_raw", [P, 2, 2 * S], U8, tag="dw_win")
        for i, words in enumerate((w1_words, w2_words)):
            nc.sync.dma_start(ww_raw[:, i, :].bitcast(I32), words[0].bitcast(I32))
        ws_raw = zeroed_bytes("ws_raw", 2 * S, nc.gpsimd, tag="dw")
        for i, scales in enumerate((w1_scales, w2_scales)):
            for q in range(4):
                nc.sync.dma_start(
                    ws_raw[32 * q:32 * q + 4, i * S:(i + 1) * S].bitcast(I32), scales[0, 4 * q:4 * q + 4, :].bitcast(I32))

        gn_safe = sb("gn_safe", [P, PACK], F32, tag="ds_dealt1")
        nc.vector.scalar_tensor_tensor(gn_safe[:], gn_sb[:], 0.0, gn_sb[:], ALU.is_equal, ALU.add)
        gn_inv = sb("gn_inv", [P, PACK], F32)
        nc.vector.reciprocal(gn_inv[:], gn_safe[:])

        z2_codes = sb("z2_codes", [P, S], I32)
        z2_scales = sb("z2_scales", [P, S], U8)
        z2 = sb("z2", [P, PACK, S], F32)
        th = []
        tab2s = []
        for t in range(PACK):
            nc.scalar.activation(ga[t][:, 0:S], a_banks[t][:], ACT.Copy, scale=gn16[:, t:t + 1])
            ga1 = sb("ga1_%d" % t, [P, S], F32)
            scalar_gather(ga1[:], ga[t], l_n1[:])
            nc.vector.scalar_tensor_tensor(z2[:, t, :], ga[t][:, rest], gm_sb[:, t:t + 1], bt[t][:], ALU.mult, ALU.add)
            tab2s.append(load_rows("tab2_", tab2, t, tag=("xw0", "ds_dealt0", "got_bytes", "xw1")[t]))
            gst = tab2s[t][:, rest]
            nc.vector.tensor_tensor(gst, ga[t][:, 0:S], ga1[:], ALU.add)
            tanh_t = sb("th%d" % t, [P, S], F32)
            nc.scalar.activation(tanh_t[:], gst, ACT.Tanh, scale=gn_inv[:, t:t + 1])
            th.append(tanh_t)
        for h, copy in enumerate((nc.vector.tensor_copy, nc.scalar.copy)):
            round_and_quantize("z2_%d" % h, z2[:, :, cols(h)], z2_codes, z2_scales, cols(h), copy)

        ww = sb("ww", [P, 2, 2 * S], U8)
        for i in range(2):
            nc.scalar.copy(
                ww[:, i, :].bitcast(U16).rearrange("p (t m) -> p t m", t=PACK),
                ww_raw[:, i, :].bitcast(U16).rearrange("p (m t) -> p t m", t=PACK),
            )
        ws = sb("ws", [P, 2 * S], U8)
        nc.vector.tensor_copy(
            ws[:].rearrange("p (w t m) -> p w t m", w=2, t=PACK),
            ws_raw[:].rearrange("p (w m t) -> p w t m", w=2, t=PACK),
        )

        h_banks = [
            [psum.tile([P, HALF], F32, name="hbank%d_%d" % (h, t), tag="bank%d" % (PACK * (1 - h) + t)) for t in range(PACK)]
            for h in range(2)
        ]

        def weight_pass(t, h, i, codes, scales, first):
            nc.tensor.matmul_mx(
                out=h_banks[h][t][:],
                lhsT=ww[:, i, 2 * P * t:2 * P * (t + 1)].bitcast(FP4X4),
                lhsT_scale=ws[:, i * S + P * t:i * S + P * (t + 1)],
                rhs=codes[:, cols(h)].bitcast(FP8X4),
                rhs_scale=scales[:, cols(h)],
                start=first, stop=not first,
            )

        for h in range(2):
            for t in range(PACK):
                weight_pass(t, h, 1, z2_codes, z2_scales, True)

        t6 = []
        for t in range(PACK):
            t6_t = sb("t6_%d" % t, [P, S], F32)
            scalar_gather(t6_t[:], tab2s[t], l_n6[:])
            t6.append(t6_t)

        z_codes = sb("z_codes", [P, S], I32)
        z_scales = sb("z_scales", [P, S], U8)
        hm = [sb("hm%d" % t, [P, S], F32) for t in range(PACK)]
        ht = [sb("ht%d" % h, [P, PACK, HALF], F32) for h in range(2)]
        for h in range(2):
            z = sb("z_%d" % h, [P, PACK, HALF], F32)
            for t in range(PACK):
                nc.vector.tensor_tensor(
                    z[:, t, :], th[t][:].indirect(half_of(l_n2, h)), tab2s[t][:, S + h * HALF:S + (h + 1) * HALF], ALU.mult)
            round_and_quantize("z%d" % h, z[:], z_codes, z_scales, cols(h), nc.vector.tensor_copy)
            for t in range(PACK):
                weight_pass(t, h, 0, z_codes, z_scales, False)
                nc.scalar.activation(hm[t][:, cols(h)], h_banks[h][t][:], ACT.Copy, scale=-0.5)
        for h in range(2):
            for t in range(PACK):
                nc.vector.scalar_tensor_tensor(
                    ht[h][:, t, :], t6[t][:, cols(h)], -2.0, hm[t][:, cols(h)], ALU.mult, ALU.mult)

        o_codes = sb("o_codes", [P, S], I32)
        o_scales = sb("o_scales", [P, S], U8)
        out_rows = out_0.rearrange("(p t) c -> p t c", t=PACK)
        words_out = out_1[0].rearrange("p c r -> p (c r)").bitcast(I32)
        for h in range(2):
            o = sb("o_%d" % h, [P, PACK, HALF], F32)
            by_scalar = (3, 2)[h]
            h7 = sb("h7_%d" % h, [P, by_scalar, HALF], F32)
            for t in range(by_scalar):
                scalar_gather(h7[:, t, :], hm[t], half_of(l_n7, h))
            for t in range(by_scalar, PACK):
                nc.vector.tensor_tensor(o[:, t, :], hm[t][:].indirect(half_of(l_n7, h)), ht[h][:, t, :], ALU.add)
            nc.vector.tensor_tensor(o[:, 0:by_scalar, :], h7[:], ht[h][:, 0:by_scalar, :], ALU.add)
            nc.sync.dma_start(out_rows[:, :, cols(h)], o[:])
            round_and_quantize("o%d" % h, o[:], o_codes, o_scales, cols(h), (nc.scalar.copy, nc.vector.tensor_copy)[h])
            nc.sync.dma_start(words_out[:, cols(h)], o_codes[:, cols(h)])
        for q in range(4):
            nc.sync.dma_start(out_2[0, 4 * q:4 * q + 4, :].bitcast(I32), o_scales[32 * q:32 * q + 4, :].bitcast(I32))
